import numpy as np
import ml_dtypes


def mxq(x, axis, fmt="e4m3"):
    dtype, down = {"e4m3": (ml_dtypes.float8_e4m3fn, 7), "e5m2": (ml_dtypes.float8_e5m2, 14)}[fmt]
    v = np.moveaxis(np.asarray(x, np.float32).astype(ml_dtypes.bfloat16).astype(np.float64), axis, -1)
    blocks = v.reshape(v.shape[:-1] + (-1, 32))
    amax = np.abs(blocks).max(-1, keepdims=True)
    byte = np.maximum(np.where(amax > 0, np.frexp(amax)[1] - 1 + 127, 0) - down, 1)
    scale = np.exp2(byte - 127.0)
    codes = (blocks / scale).astype(np.float32).astype(dtype).astype(np.float64)
    return np.moveaxis((codes * scale).reshape(v.shape), -1, axis)


WIDE = False


def mx_kscale(k):
    if not WIDE:
        return np.ones(k)
    levels = np.array([10, -10, 5, -5, 0])
    if k % 512:
        return np.exp2(np.random.permutation(np.resize(levels, k // 32))).repeat(32)
    a = np.empty((k // 512, 16))
    for p in range(k // 512):
        a[p, :8] = np.random.permutation(np.resize(levels, 8))
        for g in range(8):
            far = levels[np.abs(levels - a[p, g]) >= 10]
            a[p, g + 8] = far[np.random.randint(len(far))]
    return np.exp2(a.ravel()).repeat(32)


def f64(x):
    return np.asarray(x).astype(np.float64)


def striped(idx):
    return np.tile(idx.reshape(-1, 16).T, (8, 1)).astype(np.uint16)


def unstriped(offs):
    return offs[:16].T.reshape(-1).astype(np.int64)


def pack_weight(w):
    k, n = w.shape
    w = f64(np.asarray(w, np.float32).astype(ml_dtypes.bfloat16)).reshape(k // 32, 32, n)
    amax = np.abs(w).max(1)
    byte = np.clip(np.where(amax > 0, np.frexp(amax)[1] - 1 + 127 - 7, 1), 1, 254)
    scaled = (w * np.exp2(127.0 - byte)[:, None, :]).reshape(k, n).astype(np.float32)
    words = np.ascontiguousarray(scaled.reshape(k // 512, 128, 4, n).transpose(0, 1, 3, 2)).astype(ml_dtypes.float8_e4m3fn).view(np.uint8)
    return words, np.ascontiguousarray(byte.astype(np.uint8).reshape(k // 512, 16, n))


def unpack_weight(words, scales):
    g, p, n, _ = words.shape
    vals = np.ascontiguousarray(words).view(ml_dtypes.float8_e4m3fn).astype(np.float64) * np.repeat(np.exp2(scales.astype(np.float64) - 127.0), 8, axis=1)[..., None]
    return vals.transpose(0, 1, 3, 2).reshape(g * 512, n)


def planes(y):
    n, m = y.shape
    v = y.astype(np.float32).astype(ml_dtypes.bfloat16).astype(np.float64).reshape(n // 32, 32, m)
    top = np.abs(v).max(1)
    byte = np.clip(np.where(top > 0, np.frexp(top)[1] - 1 + 127 - 7, 1), 1, 254)
    codes = (v * np.exp2(127.0 - byte)[:, None, :]).reshape(n, m).astype(np.float32).astype(ml_dtypes.float8_e4m3fn).view(np.uint8)
    words = codes.reshape(n // 512, 128, 4, m).transpose(0, 1, 3, 2)
    return np.ascontiguousarray(words), np.ascontiguousarray(byte.astype(np.uint8).reshape(n // 512, 16, m))


def relu(v):
    return np.maximum(v, 0.0)


K, T, S, H, N = 512, 1024, 512, 512, 512


def setup_inputs():
    n = np.random.standard_normal
    s = mx_kscale(K)[:, None]
    u = mx_kscale(H)
    packed_xT = pack_weight(n((K, T)) * s)
    return {
        "x_words": packed_xT[0],
        "x_scales": packed_xT[1],
        "w1": (n((K, H)) / np.sqrt(K) / s * u).astype(np.float32),
        "w2": (n((K, N)) / np.sqrt(K) / s).astype(np.float32),
        "w3": (n((K, H)) / np.sqrt(2 * K) / s * u).astype(np.float32),
        "w4": (n((K, H)) / np.sqrt(2 * K) / s * u).astype(np.float32),
        "w5": (n((H, N)) / np.sqrt(2 * H) / u[:, None]).astype(np.float32),
        "w6": (n((H, N)) / np.sqrt(2 * H) / u[:, None]).astype(np.float32),
        "offs": striped(np.random.permutation(T)[:S]),
        "end": striped(np.random.permutation(T)[:S]),
    }


def reference(x_words, x_scales, w1, w2, w3, w4, w5, w6, offs, end):
    xq = unpack_weight(x_words, x_scales)[:, unstriped(offs)]
    y = mxq(f64(w1), 0, "e4m3").T @ xq
    x_end = unpack_weight(x_words, x_scales)[:, unstriped(end)]
    e = mxq(f64(w2), 0, "e4m3").T @ x_end
    z = y * e
    g = relu(mxq(f64(w3), 0, "e4m3").T @ xq + mxq(f64(w4), 0, "e4m3").T @ x_end)
    out_0 = mxq(f64(w5), 0, "e4m3").T @ mxq(z, 0, "e4m3") + mxq(f64(w6), 0, "e4m3").T @ mxq(g, 0, "e4m3")
    return (out_0,) + planes(out_0)

@@ -1,0 +1,254 @@
+from contextlib import ExitStack
+
+import concourse.mybir as mybir
+
+K, T, S, H, N = 512, 1024, 512, 512, 512
+FLOPS = 6 * 2 * 512 * 512 * 512
+
+F32 = mybir.dt.float32
+BF16 = mybir.dt.bfloat16
+I32 = mybir.dt.int32
+U32 = mybir.dt.uint32
+U16 = mybir.dt.uint16
+U8 = mybir.dt.uint8
+FP8X4 = mybir.dt.float8_e4m3fn_x4
+RELU = mybir.ActivationFunctionType.Relu
+MULT = mybir.AluOpType.mult
+
+P = 128
+PACK = 4
+CHUNK = 128
+CHUNKS = S // CHUNK
+
+
+def tile_picked_zspan_none_po_kernel(
+    tc, x_words, x_scales, w1, w2, w3, w4, w5, w6, offs, end, out_0, out_1, out_2
+):
+    nc = tc.nc
+    with ExitStack() as ctx:
+        lists = ctx.enter_context(tc.tile_pool(name="lists", bufs=1))
+        keep = ctx.enter_context(tc.tile_pool(name="keep", bufs=1))
+        psum = ctx.enter_context(tc.psum_pool(name="psum", bufs=1))
+
+        def sb(name, shape, dtype):
+            return keep.tile(shape, dtype, name=name, align_bytes=64)
+
+        def bank(b, shape):
+            return psum.tile(shape, F32, name="bank%d" % b, tag="bank%d" % b)
+
+        def copy(engine, out, in_):
+            if engine == "v":
+                nc.vector.tensor_copy(out=out, in_=in_)
+            else:
+                nc.scalar.copy(out=out, in_=in_)
+
+        table_scales = sb("table_scales", [P, T], U8)
+
+        offs_list = lists.tile([P, S // 16], U16, name="offs_list")
+        end_list = lists.tile([P, S // 16], U16, name="end_list")
+        table_words = sb("table_words", [P, T], U32)
+        nc.sync.dma_start(offs_list[:], offs)
+        for q in range(4):
+            (nc.scalar if q < 2 else nc.sync).dma_start(
+                out=table_scales[32 * q : 32 * q + 32, :].bitcast(I32),
+                in_=x_scales[0, 4 * q : 4 * q + 4, :].bitcast(I32).partition_broadcast(8),
+            )
+        nc.sync.dma_start(end_list[:], end)
+
+        zero = sb("zero", [P, 1], F32)
+        nc.vector.memset(zero[:], 0.0)
+        zero_bias = sb("zero_bias", [P, 1], F32)
+        nc.scalar.activation(out=zero_bias[:], in_=zero[:], func=RELU)
+
+        weights = {"w1": w1, "w2": w2, "w3": w3, "w4": w4, "w5": w5, "w6": w6}
+        pieces = {"w1":1,"w2":1,"w3":1,"w4":2,"w5":1,"w6":2}
+        raw = {}
+        loaded = []
+        for name in ["w1","w2","w3","w4","w5","w6"]:
+            rows = weights[name].rearrange("(p j) c -> p j c", j=PACK)
+            width = 512 // pieces[name]
+            raw[name] = []
+            for h in range(pieces[name]):
+                if len(loaded) == 0:
+                    nc.sync.dma_start(out=table_words[:].bitcast(I32), in_=x_words[0].rearrange("p n t -> p (n t)").bitcast(I32))
+                loaded.append(name)
+                piece = sb("raw_%s_%d" % (name, h), [P, PACK, width], F32)
+                nc.sync.dma_start(out=piece[:], in_=rows[:, :, h * width : (h + 1) * width])
+                raw[name].append(piece)
+
+        grouped = {name: sb("grouped_" + name, [P, 512 * PACK], BF16) for name in weights}
+        codes = {name: sb("codes_" + name, [P, 512], U32) for name in list(weights) + ["z", "g", "out"]}
+        scales = {name: sb("scales_" + name, [P, 512], U8) for name in list(weights) + ["z", "g", "out"]}
+
+        def cast(name, engine, m0, m1, t0, t1):
+            per = P // pieces[name]
+            h = m0 // per
+            src = raw[name][h][:].rearrange("p j (m t) -> p m j t", t=PACK)[:, m0 - h * per : m1 - h * per, :, t0:t1]
+            dst = grouped[name][:].rearrange("p (t m j) -> p m j t", t=PACK, j=PACK)[:, m0:m1, :, t0:t1]
+            copy(engine, dst, src)
+
+        def quantize(name, src, c0=0, c1=512):
+            nc.vector.quantize_mx(
+                out=codes[name][:, c0:c1].bitcast(FP8X4),
+                scales=scales[name][:, c0:c1],
+                in_=src[:, PACK * c0 : PACK * c1],
+            )
+
+        picked_words, picked_scales = {}, {}
+
+        def gather_words(name, offsets):
+            picked_words[name] = sb("words_" + name, [P, S], U32)
+            nc.vector.tensor_copy(picked_words[name][:], table_words[:].indirect(offsets[:]))
+
+        def gather_scales(name, offsets):
+            picked_scales[name] = sb("bytes_" + name, [P, S], U8)
+            nc.vector.tensor_copy(picked_scales[name][:], table_scales[:].indirect(offsets[:]))
+
+        def product(acc, name, t, words, planes, cols, start, stop):
+            stationary = slice(t * P, (t + 1) * P)
+            nc.tensor.matmul_mx(
+                out=acc,
+                lhsT=codes[name][:, stationary].bitcast(FP8X4),
+                lhsT_scale=scales[name][:, stationary],
+                rhs=words[:, cols].bitcast(FP8X4),
+                rhs_scale=planes[:, cols],
+                start=start,
+                stop=stop,
+            )
+
+        def first_layer(acc, c, terms):
+            cols = slice(c * CHUNK, (c + 1) * CHUNK)
+            for t in range(PACK):
+                for i, (name, side) in enumerate(terms):
+                    product(acc[:, t, :], name, t, picked_words[side], picked_scales[side], cols, i == 0, i == len(terms) - 1)
+
+        def woven(acc):
+            return acc[:].rearrange("p t n -> p n t")
+
+        def chunk_of(tile, c):
+            return tile[:, c * CHUNK * PACK : (c + 1) * CHUNK * PACK].rearrange("p (n t) -> p n t", t=PACK)
+
+        y_sb = [sb("y_%d" % c, [P, CHUNK * PACK], F32) for c in range(CHUNKS)]
+        z_bf = sb("z_bf", [P, S * PACK], BF16)
+        g_bf = sb("g_bf", [P, S * PACK], BF16)
+        out_half = [sb("out_f32_%d" % h, [P, PACK, S // 2], F32) for h in range(2)]
+        out_bf = sb("out_bf", [P, S * PACK], BF16)
+
+        def y_chunk(c, engine, b):
+            acc = bank(b, [P, PACK, CHUNK])
+            first_layer(acc, c, [("w1", "start")])
+            copy(engine, y_sb[c][:].rearrange("p (n t) -> p n t", t=PACK), woven(acc))
+
+        def z_chunk(c, b):
+            acc = bank(b, [P, PACK, CHUNK])
+            first_layer(acc, c, [("w2", "end")])
+            nc.vector.tensor_tensor(
+                out=chunk_of(z_bf, c), in0=woven(acc), in1=y_sb[c][:].rearrange("p (n t) -> p n t", t=PACK), op=MULT
+            )
+
+        def g_chunk(c, engine, b):
+            acc = bank(b, [P, PACK, CHUNK])
+            first_layer(acc, c, [("w3", "start"), ("w4", "end")])
+            if engine == "s":
+                nc.scalar.activation(out=chunk_of(g_bf, c), in_=woven(acc), func=RELU, bias=zero_bias[:])
+            else:
+                nc.vector.tensor_scalar_max(chunk_of(g_bf, c), woven(acc), 0.0)
+
+        def weave_out(engine, c0, c1):
+            src = out_half[c0 // 256][:, :, c0 % 256 : c0 % 256 + c1 - c0].rearrange("p t (c i) -> p c t i", i=4)
+            dst = out_bf[:, PACK * c0 : PACK * c1].rearrange("p (c i t) -> p c t i", i=4, t=PACK)
+            copy(engine, dst, src)
+
+        out_rows = out_0.rearrange("(p t) j -> p t j", t=PACK)
+        out_words = out_1[0].rearrange("p n t -> p (n t)").bitcast(I32)
+        whole = slice(0, S)
+
+        out_acc = {}
+        cast("w2", "v", 0, 128, 2, 4)
+        cast("w4", "v", 0, 64, 0, 4)
+        gather_scales("start", offs_list)
+        gather_scales("end", end_list)
+        gather_words("start", offs_list)
+        gather_words("end", end_list)
+        cast("w1", "s", 0, 128, 2, 4)
+        cast("w4", "s", 64, 128, 0, 4)
+        cast("w2", "v", 0, 128, 0, 2)
+        cast("w3", "v", 0, 128, 0, 4)
+        cast("w1", "s", 0, 128, 0, 2)
+        quantize("w1", grouped["w1"], 0, 256)
+        cast("w6", "s", 0, 64, 2, 4)
+        quantize("w4", grouped["w4"], 256, 512)
+        quantize("w1", grouped["w1"], 256, 512)
+        cast("w6", "v", 0, 64, 0, 2)
+        quantize("w4", grouped["w4"], 0, 256)
+        cast("w5", "s", 0, 128, 0, 4)
+        quantize("w3", grouped["w3"], 256, 512)
+        quantize("w2", grouped["w2"])
+        y_chunk(0, "s", 0)
+        y_chunk(3, "s", 1)
+        quantize("w3", grouped["w3"], 0, 256)
+        y_chunk(1, "s", 2)
+        z_chunk(0, 3)
+        g_chunk(3, "s", 4)
+        z_chunk(3, 5)
+        g_chunk(2, "s", 6)
+        y_chunk(2, "s", 7)
+        z_chunk(1, 0)
+        cast("w6", "v", 64, 128, 0, 4)
+        z_chunk(2, 1)
+        quantize("w5", grouped["w5"])
+        quantize("g", g_bf, 256, 512)
+        g_chunk(1, "s", 2)
+        g_chunk(0, "s", 3)
+        quantize("w6", grouped["w6"], 256, 384)
+        quantize("w6", grouped["w6"], 384, 512)
+        quantize("w6", grouped["w6"], 0, 128)
+        quantize("w6", grouped["w6"], 128, 256)
+        quantize("z", z_bf, 0, 256)
+        quantize("z", z_bf, 256, 512)
+        out_acc[0, 0] = bank(4, [P, 256])
+        product(out_acc[0, 0][:], "w5", 0, codes["z"], scales["z"], slice(0, 256), True, False)
+        out_acc[1, 0] = bank(5, [P, 256])
+        product(out_acc[1, 0][:], "w5", 1, codes["z"], scales["z"], slice(0, 256), True, False)
+        out_acc[2, 0] = bank(6, [P, 256])
+        product(out_acc[2, 0][:], "w5", 2, codes["z"], scales["z"], slice(0, 256), True, False)
+        out_acc[3, 0] = bank(7, [P, 256])
+        product(out_acc[3, 0][:], "w5", 3, codes["z"], scales["z"], slice(0, 256), True, False)
+        out_acc[0, 256] = bank(0, [P, 256])
+        product(out_acc[0, 256][:], "w5", 0, codes["z"], scales["z"], slice(256, 512), True, False)
+        out_acc[1, 256] = bank(1, [P, 256])
+        product(out_acc[1, 256][:], "w5", 1, codes["z"], scales["z"], slice(256, 512), True, False)
+        out_acc[2, 256] = bank(2, [P, 256])
+        product(out_acc[2, 256][:], "w5", 2, codes["z"], scales["z"], slice(256, 512), True, False)
+        out_acc[3, 256] = bank(3, [P, 256])
+        product(out_acc[3, 256][:], "w5", 3, codes["z"], scales["z"], slice(256, 512), True, False)
+        quantize("g", g_bf, 0, 256)
+        product(out_acc[0, 0][:], "w6", 0, codes["g"], scales["g"], slice(0, 256), False, True)
+        product(out_acc[1, 0][:], "w6", 1, codes["g"], scales["g"], slice(0, 256), False, True)
+        product(out_acc[2, 0][:], "w6", 2, codes["g"], scales["g"], slice(0, 256), False, True)
+        product(out_acc[3, 0][:], "w6", 3, codes["g"], scales["g"], slice(0, 256), False, True)
+        copy("s", out_half[0][:, 0, 0:256], out_acc[0, 0][:])
+        copy("v", out_half[0][:, 1, 0:256], out_acc[1, 0][:])
+        copy("s", out_half[0][:, 2, 0:256], out_acc[2, 0][:])
+        copy("v", out_half[0][:, 3, 0:256], out_acc[3, 0][:])
+        nc.sync.dma_start(out=out_rows[:, 0:4, 0:256], in_=out_half[0][:, 0:4, 0:256])
+        product(out_acc[0, 256][:], "w6", 0, codes["g"], scales["g"], slice(256, 512), False, True)
+        product(out_acc[1, 256][:], "w6", 1, codes["g"], scales["g"], slice(256, 512), False, True)
+        product(out_acc[2, 256][:], "w6", 2, codes["g"], scales["g"], slice(256, 512), False, True)
+        product(out_acc[3, 256][:], "w6", 3, codes["g"], scales["g"], slice(256, 512), False, True)
+        weave_out("v", 0, 256)
+        quantize("out", out_bf, 0, 256)
+        nc.sync.dma_start(out=out_words[:, 0:256], in_=codes["out"][:, 0:256].bitcast(I32))
+        copy("v", out_half[1][:, 0, 0:256], out_acc[0, 256][:])
+        copy("v", out_half[1][:, 1, 0:256], out_acc[1, 256][:])
+        copy("s", out_half[1][:, 2, 0:256], out_acc[2, 256][:])
+        copy("s", out_half[1][:, 3, 0:256], out_acc[3, 256][:])
+        nc.sync.dma_start(out=out_rows[:, 0:4, 256:512], in_=out_half[1][:, 0:4, 0:256])
+        weave_out("v", 256, 320)
+        weave_out("s", 320, 512)
+        quantize("out", out_bf, 256, 512)
+        nc.sync.dma_start(out=out_words[:, 256:512], in_=codes["out"][:, 256:512].bitcast(I32))
+        nc.scalar.dma_start(out=out_2[0, 0:4, :].bitcast(I32), in_=scales["out"][0:4, :].bitcast(I32))
+        nc.sync.dma_start(out=out_2[0, 4:8, :].bitcast(I32), in_=scales["out"][32:36, :].bitcast(I32))
+        nc.scalar.dma_start(out=out_2[0, 8:12, :].bitcast(I32), in_=scales["out"][64:68, :].bitcast(I32))
+        nc.sync.dma_start(out=out_2[0, 12:16, :].bitcast(I32), in_=scales["out"][96:100, :].bitcast(I32))

@@ -61,7 +61,7 @@ def tile_picked_zspan_none_po_kernel(
         nc.scalar.activation(out=zero_bias[:], in_=zero[:], func=RELU)
 
         weights = {"w1": w1, "w2": w2, "w3": w3, "w4": w4, "w5": w5, "w6": w6}
-        pieces = {"w1":1,"w2":1,"w3":1,"w4":2,"w5":1,"w6":2}
+        pieces = {"w1":1,"w2":1,"w3":1,"w4":1,"w5":1,"w6":2}
         raw = {}
         loaded = []
         for name in ["w1","w2","w3","w4","w5","w6"]:
@@ -154,6 +154,34 @@ def tile_picked_zspan_none_po_kernel(
             else:
                 nc.vector.tensor_scalar_max(chunk_of(g_bf, c), woven(acc), 0.0)
 
+        held = {}
+        out_part = []
+
+        def passes(acc, kind, c, name, first):
+            cols = slice(c * CHUNK, (c + 1) * CHUNK)
+            if kind == "g":
+                side = "start" if name == "w3" else "end"
+                words, planes = picked_words[side], picked_scales[side]
+            else:
+                src = "z" if name == "w5" else "g"
+                words, planes = codes[src], scales[src]
+            for t in range(PACK):
+                product(acc[:, t, :], name, t, words, planes, cols, first and t == 0, (not first) and t == PACK - 1)
+
+        def open_group(kind, c, name, b):
+            held[kind, c] = bank(b, [P, PACK, CHUNK])
+            passes(held[kind, c], kind, c, name, True)
+
+        def close_group(kind, c, name, engine):
+            acc = held[kind, c]
+            passes(acc, kind, c, name, False)
+            if kind == "o":
+                copy(engine, out_part[c][:], acc[:])
+            elif engine == "s":
+                nc.scalar.activation(out=chunk_of(g_bf, c), in_=woven(acc), func=RELU, bias=zero_bias[:])
+            else:
+                nc.vector.tensor_scalar_max(chunk_of(g_bf, c), woven(acc), 0.0)
+
         def weave_out(engine, c0, c1):
             src = out_half[c0 // 256][:, :, c0 % 256 : c0 % 256 + c1 - c0].rearrange("p t (c i) -> p c t i", i=4)
             dst = out_bf[:, PACK * c0 : PACK * c1].rearrange("p (c i t) -> p c t i", i=4, t=PACK)
@@ -164,88 +192,97 @@ def tile_picked_zspan_none_po_kernel(
         whole = slice(0, S)
 
         out_acc = {}
+        cast("w3", "v", 32, 128, 0, 4)
+        cast("w3", "s", 0, 32, 0, 4)
+        cast("w5", "s", 0, 64, 2, 4)
+        cast("w5", "v", 64, 128, 2, 4)
+        cast("w6", "v", 0, 64, 0, 4)
+        cast("w1", "s", 0, 64, 2, 4)
+        cast("w1", "v", 64, 128, 2, 4)
         cast("w2", "v", 0, 128, 2, 4)
-        cast("w4", "v", 0, 64, 0, 4)
-        gather_scales("start", offs_list)
-        gather_scales("end", end_list)
-        gather_words("start", offs_list)
-        gather_words("end", end_list)
-        cast("w1", "s", 0, 128, 2, 4)
-        cast("w4", "s", 64, 128, 0, 4)
-        cast("w2", "v", 0, 128, 0, 2)
-        cast("w3", "v", 0, 128, 0, 4)
+        cast("w5", "s", 0, 128, 0, 2)
+        cast("w4", "s", 0, 128, 0, 2)
+        cast("w4", "v", 96, 128, 2, 4)
+        cast("w4", "s", 0, 96, 2, 4)
+        cast("w2", "s", 0, 128, 0, 2)
         cast("w1", "s", 0, 128, 0, 2)
         quantize("w1", grouped["w1"], 0, 256)
-        cast("w6", "s", 0, 64, 2, 4)
-        quantize("w4", grouped["w4"], 256, 512)
+        gather_scales("end", end_list)
+        quantize("w3", grouped["w3"])
+        quantize("w4", grouped["w4"])
         quantize("w1", grouped["w1"], 256, 512)
-        cast("w6", "v", 0, 64, 0, 2)
-        quantize("w4", grouped["w4"], 0, 256)
-        cast("w5", "s", 0, 128, 0, 4)
-        quantize("w3", grouped["w3"], 256, 512)
-        quantize("w2", grouped["w2"])
-        y_chunk(0, "s", 0)
-        y_chunk(3, "s", 1)
-        quantize("w3", grouped["w3"], 0, 256)
-        y_chunk(1, "s", 2)
-        z_chunk(0, 3)
-        g_chunk(3, "s", 4)
-        z_chunk(3, 5)
-        g_chunk(2, "s", 6)
-        y_chunk(2, "s", 7)
-        z_chunk(1, 0)
+        gather_words("start", offs_list)
+        gather_scales("start", offs_list)
+        gather_words("end", end_list)
+        y_chunk(2, "s", 0)
+        y_chunk(0, "s", 1)
+        open_group("g", 1, "w3", 2)
+        y_chunk(1, "s", 3)
         cast("w6", "v", 64, 128, 0, 4)
-        z_chunk(2, 1)
-        quantize("w5", grouped["w5"])
-        quantize("g", g_bf, 256, 512)
-        g_chunk(1, "s", 2)
-        g_chunk(0, "s", 3)
-        quantize("w6", grouped["w6"], 256, 384)
-        quantize("w6", grouped["w6"], 384, 512)
+        quantize("w2", grouped["w2"], 0, 128)
+        quantize("w2", grouped["w2"], 128, 256)
+        quantize("w2", grouped["w2"], 256, 384)
+        quantize("w2", grouped["w2"], 384, 512)
+        y_chunk(3, "s", 4)
+        open_group("g", 0, "w3", 5)
+        open_group("g", 3, "w3", 6)
         quantize("w6", grouped["w6"], 0, 128)
         quantize("w6", grouped["w6"], 128, 256)
-        quantize("z", z_bf, 0, 256)
+        open_group("g", 2, "w3", 7)
+        z_chunk(1, 0)
+        quantize("w5", grouped["w5"])
+        close_group("g", 0, "w4", "s")
+        z_chunk(2, 1)
+        close_group("g", 1, "w4", "s")
+        close_group("g", 3, "w4", "s")
+        quantize("g", g_bf, 0, 256)
+        quantize("w6", grouped["w6"], 256, 384)
+        quantize("w6", grouped["w6"], 384, 512)
+        z_chunk(3, 3)
+        z_chunk(0, 4)
+        close_group("g", 2, "w4", "s")
         quantize("z", z_bf, 256, 512)
-        out_acc[0, 0] = bank(4, [P, 256])
+        quantize("z", z_bf, 0, 256)
+        quantize("g", g_bf, 256, 512)
+        out_acc[0, 0] = bank(0, [P, 256])
         product(out_acc[0, 0][:], "w5", 0, codes["z"], scales["z"], slice(0, 256), True, False)
         out_acc[1, 0] = bank(5, [P, 256])
         product(out_acc[1, 0][:], "w5", 1, codes["z"], scales["z"], slice(0, 256), True, False)
-        out_acc[2, 0] = bank(6, [P, 256])
+        out_acc[2, 0] = bank(1, [P, 256])
         product(out_acc[2, 0][:], "w5", 2, codes["z"], scales["z"], slice(0, 256), True, False)
-        out_acc[3, 0] = bank(7, [P, 256])
+        out_acc[3, 0] = bank(2, [P, 256])
         product(out_acc[3, 0][:], "w5", 3, codes["z"], scales["z"], slice(0, 256), True, False)
-        out_acc[0, 256] = bank(0, [P, 256])
+        out_acc[0, 256] = bank(6, [P, 256])
         product(out_acc[0, 256][:], "w5", 0, codes["z"], scales["z"], slice(256, 512), True, False)
-        out_acc[1, 256] = bank(1, [P, 256])
+        out_acc[1, 256] = bank(3, [P, 256])
         product(out_acc[1, 256][:], "w5", 1, codes["z"], scales["z"], slice(256, 512), True, False)
-        out_acc[2, 256] = bank(2, [P, 256])
+        out_acc[2, 256] = bank(4, [P, 256])
         product(out_acc[2, 256][:], "w5", 2, codes["z"], scales["z"], slice(256, 512), True, False)
-        out_acc[3, 256] = bank(3, [P, 256])
+        out_acc[3, 256] = bank(7, [P, 256])
         product(out_acc[3, 256][:], "w5", 3, codes["z"], scales["z"], slice(256, 512), True, False)
-        quantize("g", g_bf, 0, 256)
-        product(out_acc[0, 0][:], "w6", 0, codes["g"], scales["g"], slice(0, 256), False, True)
-        product(out_acc[1, 0][:], "w6", 1, codes["g"], scales["g"], slice(0, 256), False, True)
-        product(out_acc[2, 0][:], "w6", 2, codes["g"], scales["g"], slice(0, 256), False, True)
-        product(out_acc[3, 0][:], "w6", 3, codes["g"], scales["g"], slice(0, 256), False, True)
-        copy("s", out_half[0][:, 0, 0:256], out_acc[0, 0][:])
-        copy("v", out_half[0][:, 1, 0:256], out_acc[1, 0][:])
-        copy("s", out_half[0][:, 2, 0:256], out_acc[2, 0][:])
-        copy("v", out_half[0][:, 3, 0:256], out_acc[3, 0][:])
-        nc.sync.dma_start(out=out_rows[:, 0:4, 0:256], in_=out_half[0][:, 0:4, 0:256])
         product(out_acc[0, 256][:], "w6", 0, codes["g"], scales["g"], slice(256, 512), False, True)
         product(out_acc[1, 256][:], "w6", 1, codes["g"], scales["g"], slice(256, 512), False, True)
         product(out_acc[2, 256][:], "w6", 2, codes["g"], scales["g"], slice(256, 512), False, True)
         product(out_acc[3, 256][:], "w6", 3, codes["g"], scales["g"], slice(256, 512), False, True)
+        product(out_acc[0, 0][:], "w6", 0, codes["g"], scales["g"], slice(0, 256), False, True)
+        product(out_acc[1, 0][:], "w6", 1, codes["g"], scales["g"], slice(0, 256), False, True)
+        product(out_acc[2, 0][:], "w6", 2, codes["g"], scales["g"], slice(0, 256), False, True)
+        product(out_acc[3, 0][:], "w6", 3, codes["g"], scales["g"], slice(0, 256), False, True)
+        copy("v", out_half[1][:, 0, 0:256], out_acc[0, 256][:])
+        copy("s", out_half[1][:, 1, 0:256], out_acc[1, 256][:])
+        copy("v", out_half[1][:, 2, 0:256], out_acc[2, 256][:])
+        copy("s", out_half[1][:, 3, 0:256], out_acc[3, 256][:])
+        nc.sync.dma_start(out=out_rows[:, 0:4, 256:512], in_=out_half[1][:, 0:4, 0:256])
+        copy("s", out_half[0][:, 0, 0:256], out_acc[0, 0][:])
+        copy("s", out_half[0][:, 1, 0:256], out_acc[1, 0][:])
+        copy("v", out_half[0][:, 2, 0:256], out_acc[2, 0][:])
+        copy("s", out_half[0][:, 3, 0:256], out_acc[3, 0][:])
+        nc.sync.dma_start(out=out_rows[:, 0:4, 0:256], in_=out_half[0][:, 0:4, 0:256])
         weave_out("v", 0, 256)
         quantize("out", out_bf, 0, 256)
         nc.sync.dma_start(out=out_words[:, 0:256], in_=codes["out"][:, 0:256].bitcast(I32))
-        copy("v", out_half[1][:, 0, 0:256], out_acc[0, 256][:])
-        copy("v", out_half[1][:, 1, 0:256], out_acc[1, 256][:])
-        copy("s", out_half[1][:, 2, 0:256], out_acc[2, 256][:])
-        copy("s", out_half[1][:, 3, 0:256], out_acc[3, 256][:])
-        nc.sync.dma_start(out=out_rows[:, 0:4, 256:512], in_=out_half[1][:, 0:4, 0:256])
-        weave_out("v", 256, 320)
-        weave_out("s", 320, 512)
+        weave_out("v", 256, 384)
+        weave_out("s", 384, 512)
         quantize("out", out_bf, 256, 512)
         nc.sync.dma_start(out=out_words[:, 256:512], in_=codes["out"][:, 256:512].bitcast(I32))
         nc.scalar.dma_start(out=out_2[0, 0:4, :].bitcast(I32), in_=scales["out"][0:4, :].bitcast(I32))

@@ -2,8 +2,10 @@ from contextlib import ExitStack
 
 import concourse.mybir as mybir
 
-K, T, S, H, N = 512, 1024, 512, 512, 512
-FLOPS = 6 * 2 * 512 * 512 * 512
+TOKENS = 1024
+SPANS = 512
+WIDTH = 512
+FLOPS = 6 * 2 * WIDTH * WIDTH * SPANS
 
 F32 = mybir.dt.float32
 BF16 = mybir.dt.bfloat16
@@ -17,275 +19,203 @@ MULT = mybir.AluOpType.mult
 
 P = 128
 PACK = 4
+QUADRANTS = 4
 CHUNK = 128
-CHUNKS = S // CHUNK
+CHUNKS = SPANS // CHUNK
+HALF = SPANS // 2
+
+PIECES = {"w1": 1, "w2": 1, "w3": 2, "w4": 1, "w5": 1, "w6": 2}
+SCALAR_SHARE = {"w1": 64, "w2": 0, "w4": 96, "w5": 64}
+VECTOR_WEAVES = (256, 160)
+EMPTIED_BY = ("svsv", "svss")
+STORE_GROUPS = (2, 4)
 
 
 def tile_picked_zspan_none_po_kernel(
     tc, x_words, x_scales, w1, w2, w3, w4, w5, w6, offs, end, out_0, out_1, out_2
 ):
     nc = tc.nc
+    vector_copy = nc.vector.tensor_copy
+    scalar_copy = nc.scalar.copy
+
     with ExitStack() as ctx:
         lists = ctx.enter_context(tc.tile_pool(name="lists", bufs=1))
         keep = ctx.enter_context(tc.tile_pool(name="keep", bufs=1))
         psum = ctx.enter_context(tc.psum_pool(name="psum", bufs=1))
 
-        def sb(name, shape, dtype):
+        def sbuf(name, shape, dtype):
             return keep.tile(shape, dtype, name=name, align_bytes=64)
 
         def bank(b, shape):
             return psum.tile(shape, F32, name="bank%d" % b, tag="bank%d" % b)
 
-        def copy(engine, out, in_):
-            if engine == "v":
-                nc.vector.tensor_copy(out=out, in_=in_)
-            else:
-                nc.scalar.copy(out=out, in_=in_)
+        list_tiles = {side: lists.tile([P, SPANS // 16], U16, name="list_" + side) for side in ("start", "end")}
+        table_scales = sbuf("table_scales", [P, TOKENS], U8)
+        table_words = sbuf("table_words", [P, TOKENS], U32)
+        weights = {"w1": w1, "w2": w2, "w3": w3, "w4": w4, "w5": w5, "w6": w6}
+        raw = {name: [] for name in weights}
 
-        table_scales = sb("table_scales", [P, T], U8)
+        def load_piece(name, h):
+            width = WIDTH // PIECES[name]
+            piece = sbuf("raw_%s_%d" % (name, h), [P, PACK, width], F32)
+            rows = weights[name].rearrange("(p j) c -> p j c", j=PACK)
+            nc.sync.dma_start(out=piece[:], in_=rows[:, :, h * width : (h + 1) * width])
+            raw[name].append(piece)
 
-        offs_list = lists.tile([P, S // 16], U16, name="offs_list")
-        end_list = lists.tile([P, S // 16], U16, name="end_list")
-        table_words = sb("table_words", [P, T], U32)
-        nc.sync.dma_start(offs_list[:], offs)
-        for q in range(4):
-            (nc.scalar if q < 2 else nc.sync).dma_start(
+        nc.sync.dma_start(list_tiles["start"][:], offs)
+        for q in range(QUADRANTS):
+            (nc.scalar if q < QUADRANTS // 2 else nc.sync).dma_start(
                 out=table_scales[32 * q : 32 * q + 32, :].bitcast(I32),
                 in_=x_scales[0, 4 * q : 4 * q + 4, :].bitcast(I32).partition_broadcast(8),
             )
-        nc.sync.dma_start(end_list[:], end)
-
-        zero = sb("zero", [P, 1], F32)
+        nc.sync.dma_start(list_tiles["end"][:], end)
+        zero = sbuf("zero", [P, 1], F32)
         nc.vector.memset(zero[:], 0.0)
-        zero_bias = sb("zero_bias", [P, 1], F32)
+        zero_bias = sbuf("zero_bias", [P, 1], F32)
         nc.scalar.activation(out=zero_bias[:], in_=zero[:], func=RELU)
 
-        weights = {"w1": w1, "w2": w2, "w3": w3, "w4": w4, "w5": w5, "w6": w6}
-        pieces = {"w1":1,"w2":1,"w3":1,"w4":1,"w5":1,"w6":2}
-        raw = {}
-        loaded = []
-        for name in ["w1","w2","w3","w4","w5","w6"]:
-            rows = weights[name].rearrange("(p j) c -> p j c", j=PACK)
-            width = 512 // pieces[name]
-            raw[name] = []
-            for h in range(pieces[name]):
-                if len(loaded) == 0:
-                    nc.sync.dma_start(out=table_words[:].bitcast(I32), in_=x_words[0].rearrange("p n t -> p (n t)").bitcast(I32))
-                loaded.append(name)
-                piece = sb("raw_%s_%d" % (name, h), [P, PACK, width], F32)
-                nc.sync.dma_start(out=piece[:], in_=rows[:, :, h * width : (h + 1) * width])
-                raw[name].append(piece)
+        nc.sync.dma_start(out=table_words[:].bitcast(I32), in_=x_words[0].rearrange("p n t -> p (n t)").bitcast(I32))
+        for name in weights:
+            for h in range(PIECES[name]):
+                load_piece(name, h)
 
-        grouped = {name: sb("grouped_" + name, [P, 512 * PACK], BF16) for name in weights}
-        codes = {name: sb("codes_" + name, [P, 512], U32) for name in list(weights) + ["z", "g", "out"]}
-        scales = {name: sb("scales_" + name, [P, 512], U8) for name in list(weights) + ["z", "g", "out"]}
+        made_here = list(weights) + ["z", "g", "out"]
+        woven = {name: sbuf("woven_" + name, [P, WIDTH * PACK], BF16) for name in made_here}
+        words = {name: sbuf("words_" + name, [P, WIDTH], U32) for name in made_here + ["start", "end"]}
+        scales = {name: sbuf("scales_" + name, [P, WIDTH], U8) for name in made_here + ["start", "end"]}
 
-        def cast(name, engine, m0, m1, t0, t1):
-            per = P // pieces[name]
+        def round_part(name, copy, m0, m1, t0, t1):
+            per = P // PIECES[name]
             h = m0 // per
-            src = raw[name][h][:].rearrange("p j (m t) -> p m j t", t=PACK)[:, m0 - h * per : m1 - h * per, :, t0:t1]
-            dst = grouped[name][:].rearrange("p (t m j) -> p m j t", t=PACK, j=PACK)[:, m0:m1, :, t0:t1]
-            copy(engine, dst, src)
+            src = raw[name][h][:].rearrange("p j (m t) -> p m j t", t=PACK)
+            dst = woven[name][:].rearrange("p (t m j) -> p m j t", t=PACK, j=PACK)
+            copy(out=dst[:, m0:m1, :, t0:t1], in_=src[:, m0 - h * per : m1 - h * per, :, t0:t1])
 
-        def quantize(name, src, c0=0, c1=512):
+        def round_on_vector(name):
+            per = P // PIECES[name]
+            for m0 in range(0, P, per):
+                round_part(name, vector_copy, m0, m0 + per, 0, PACK)
+
+        def round_shared(name):
+            share = SCALAR_SHARE[name]
+            if share:
+                round_part(name, scalar_copy, 0, share, 2, PACK)
+            round_part(name, vector_copy, share, P, 2, PACK)
+            round_part(name, scalar_copy, 0, P, 0, 2)
+
+        def quantize(name, c0=0, c1=WIDTH):
             nc.vector.quantize_mx(
-                out=codes[name][:, c0:c1].bitcast(FP8X4),
+                out=words[name][:, c0:c1].bitcast(FP8X4),
                 scales=scales[name][:, c0:c1],
-                in_=src[:, PACK * c0 : PACK * c1],
+                in_=woven[name][:, PACK * c0 : PACK * c1],
             )
 
-        picked_words, picked_scales = {}, {}
+        def quantize_pairs(name, order):
+            for pair in order:
+                quantize(name, pair * 2 * P, (pair + 1) * 2 * P)
 
-        def gather_words(name, offsets):
-            picked_words[name] = sb("words_" + name, [P, S], U32)
-            nc.vector.tensor_copy(picked_words[name][:], table_words[:].indirect(offsets[:]))
-
-        def gather_scales(name, offsets):
-            picked_scales[name] = sb("bytes_" + name, [P, S], U8)
-            nc.vector.tensor_copy(picked_scales[name][:], table_scales[:].indirect(offsets[:]))
-
-        def product(acc, name, t, words, planes, cols, start, stop):
-            stationary = slice(t * P, (t + 1) * P)
+        def product(acc, weight, t, moving, cols, start, stop):
+            group = slice(t * P, (t + 1) * P)
             nc.tensor.matmul_mx(
                 out=acc,
-                lhsT=codes[name][:, stationary].bitcast(FP8X4),
-                lhsT_scale=scales[name][:, stationary],
-                rhs=words[:, cols].bitcast(FP8X4),
-                rhs_scale=planes[:, cols],
+                lhsT=words[weight][:, group].bitcast(FP8X4),
+                lhsT_scale=scales[weight][:, group],
+                rhs=words[moving][:, cols].bitcast(FP8X4),
+                rhs_scale=scales[moving][:, cols],
                 start=start,
                 stop=stop,
             )
 
-        def first_layer(acc, c, terms):
-            cols = slice(c * CHUNK, (c + 1) * CHUNK)
-            for t in range(PACK):
-                for i, (name, side) in enumerate(terms):
-                    product(acc[:, t, :], name, t, picked_words[side], picked_scales[side], cols, i == 0, i == len(terms) - 1)
+        def chunk_cols(c):
+            return slice(c * CHUNK, (c + 1) * CHUNK)
 
-        def woven(acc):
+        def weaving_read(acc):
             return acc[:].rearrange("p t n -> p n t")
 
-        def chunk_of(tile, c):
-            return tile[:, c * CHUNK * PACK : (c + 1) * CHUNK * PACK].rearrange("p (n t) -> p n t", t=PACK)
+        def woven_chunk(tile, c):
+            return tile[:, PACK * CHUNK * c : PACK * CHUNK * (c + 1)].rearrange("p (n t) -> p n t", t=PACK)
 
-        y_sb = [sb("y_%d" % c, [P, CHUNK * PACK], F32) for c in range(CHUNKS)]
-        z_bf = sb("z_bf", [P, S * PACK], BF16)
-        g_bf = sb("g_bf", [P, S * PACK], BF16)
-        out_half = [sb("out_f32_%d" % h, [P, PACK, S // 2], F32) for h in range(2)]
-        out_bf = sb("out_bf", [P, S * PACK], BF16)
+        for side in ("start", "end"):
+            nc.vector.tensor_copy(scales[side][:], table_scales[:].indirect(list_tiles[side][:]))
+            nc.vector.tensor_copy(words[side][:], table_words[:].indirect(list_tiles[side][:]))
 
-        def y_chunk(c, engine, b):
-            acc = bank(b, [P, PACK, CHUNK])
-            first_layer(acc, c, [("w1", "start")])
-            copy(engine, y_sb[c][:].rearrange("p (n t) -> p n t", t=PACK), woven(acc))
+        for name in weights:
+            if name in SCALAR_SHARE:
+                round_shared(name)
+            else:
+                round_on_vector(name)
+            quantize_pairs(name, (1, 0))
 
-        def z_chunk(c, b):
-            acc = bank(b, [P, PACK, CHUNK])
-            first_layer(acc, c, [("w2", "end")])
+        y_chunks = [sbuf("y_%d" % c, [P, PACK * CHUNK], F32) for c in range(CHUNKS)]
+        for c in range(CHUNKS):
+            acc = bank(c, [P, PACK, CHUNK])
+            for t in range(PACK):
+                product(acc[:, t, :], "w1", t, "start", chunk_cols(c), True, True)
+            nc.scalar.copy(out=woven_chunk(y_chunks[c], 0), in_=weaving_read(acc))
+
+        g_banks = [bank(CHUNKS + c, [P, PACK, CHUNK]) for c in range(CHUNKS)]
+        for c in range(CHUNKS):
+            for t in range(PACK):
+                product(g_banks[c][:, t, :], "w3", t, "start", chunk_cols(c), t == 0, False)
+
+        for c in range(CHUNKS):
+            acc = bank(c, [P, PACK, CHUNK])
+            for t in range(PACK):
+                product(acc[:, t, :], "w2", t, "end", chunk_cols(c), True, True)
             nc.vector.tensor_tensor(
-                out=chunk_of(z_bf, c), in0=woven(acc), in1=y_sb[c][:].rearrange("p (n t) -> p n t", t=PACK), op=MULT
+                out=woven_chunk(woven["z"], c), in0=weaving_read(acc), in1=woven_chunk(y_chunks[c], 0), op=MULT
             )
 
-        def g_chunk(c, engine, b):
-            acc = bank(b, [P, PACK, CHUNK])
-            first_layer(acc, c, [("w3", "start"), ("w4", "end")])
-            if engine == "s":
-                nc.scalar.activation(out=chunk_of(g_bf, c), in_=woven(acc), func=RELU, bias=zero_bias[:])
-            else:
-                nc.vector.tensor_scalar_max(chunk_of(g_bf, c), woven(acc), 0.0)
+        halves = [slice(0, HALF), slice(HALF, SPANS)]
+        for cols in halves:
+            quantize("z", cols.start, cols.stop)
 
-        held = {}
-        out_part = []
-
-        def passes(acc, kind, c, name, first):
-            cols = slice(c * CHUNK, (c + 1) * CHUNK)
-            if kind == "g":
-                side = "start" if name == "w3" else "end"
-                words, planes = picked_words[side], picked_scales[side]
-            else:
-                src = "z" if name == "w5" else "g"
-                words, planes = codes[src], scales[src]
+        for c in range(CHUNKS):
             for t in range(PACK):
-                product(acc[:, t, :], name, t, words, planes, cols, first and t == 0, (not first) and t == PACK - 1)
+                product(g_banks[c][:, t, :], "w4", t, "end", chunk_cols(c), False, t == PACK - 1)
+            nc.scalar.activation(
+                out=woven_chunk(woven["g"], c), in_=weaving_read(g_banks[c]), func=RELU, bias=zero_bias[:]
+            )
 
-        def open_group(kind, c, name, b):
-            held[kind, c] = bank(b, [P, PACK, CHUNK])
-            passes(held[kind, c], kind, c, name, True)
+        for cols in halves:
+            quantize("g", cols.start, cols.stop)
 
-        def close_group(kind, c, name, engine):
-            acc = held[kind, c]
-            passes(acc, kind, c, name, False)
-            if kind == "o":
-                copy(engine, out_part[c][:], acc[:])
-            elif engine == "s":
-                nc.scalar.activation(out=chunk_of(g_bf, c), in_=woven(acc), func=RELU, bias=zero_bias[:])
-            else:
-                nc.vector.tensor_scalar_max(chunk_of(g_bf, c), woven(acc), 0.0)
-
-        def weave_out(engine, c0, c1):
-            src = out_half[c0 // 256][:, :, c0 % 256 : c0 % 256 + c1 - c0].rearrange("p t (c i) -> p c t i", i=4)
-            dst = out_bf[:, PACK * c0 : PACK * c1].rearrange("p (c i t) -> p c t i", i=4, t=PACK)
-            copy(engine, dst, src)
-
+        out_banks = [[bank(PACK * h + t, [P, HALF]) for t in range(PACK)] for h in range(2)]
         out_rows = out_0.rearrange("(p t) j -> p t j", t=PACK)
-        out_words = out_1[0].rearrange("p n t -> p (n t)").bitcast(I32)
-        whole = slice(0, S)
+        out_halves = [sbuf("out_f32_%d" % h, [P, PACK, HALF], F32) for h in range(2)]
 
-        out_acc = {}
-        cast("w3", "v", 32, 128, 0, 4)
-        cast("w3", "s", 0, 32, 0, 4)
-        cast("w5", "s", 0, 64, 2, 4)
-        cast("w5", "v", 64, 128, 2, 4)
-        cast("w6", "v", 0, 64, 0, 4)
-        cast("w1", "s", 0, 64, 2, 4)
-        cast("w1", "v", 64, 128, 2, 4)
-        cast("w2", "v", 0, 128, 2, 4)
-        cast("w5", "s", 0, 128, 0, 2)
-        cast("w4", "s", 0, 128, 0, 2)
-        cast("w4", "v", 96, 128, 2, 4)
-        cast("w4", "s", 0, 96, 2, 4)
-        cast("w2", "s", 0, 128, 0, 2)
-        cast("w1", "s", 0, 128, 0, 2)
-        quantize("w1", grouped["w1"], 0, 256)
-        gather_scales("end", end_list)
-        quantize("w3", grouped["w3"])
-        quantize("w4", grouped["w4"])
-        quantize("w1", grouped["w1"], 256, 512)
-        gather_words("start", offs_list)
-        gather_scales("start", offs_list)
-        gather_words("end", end_list)
-        y_chunk(2, "s", 0)
-        y_chunk(0, "s", 1)
-        open_group("g", 1, "w3", 2)
-        y_chunk(1, "s", 3)
-        cast("w6", "v", 64, 128, 0, 4)
-        quantize("w2", grouped["w2"], 0, 128)
-        quantize("w2", grouped["w2"], 128, 256)
-        quantize("w2", grouped["w2"], 256, 384)
-        quantize("w2", grouped["w2"], 384, 512)
-        y_chunk(3, "s", 4)
-        open_group("g", 0, "w3", 5)
-        open_group("g", 3, "w3", 6)
-        quantize("w6", grouped["w6"], 0, 128)
-        quantize("w6", grouped["w6"], 128, 256)
-        open_group("g", 2, "w3", 7)
-        z_chunk(1, 0)
-        quantize("w5", grouped["w5"])
-        close_group("g", 0, "w4", "s")
-        z_chunk(2, 1)
-        close_group("g", 1, "w4", "s")
-        close_group("g", 3, "w4", "s")
-        quantize("g", g_bf, 0, 256)
-        quantize("w6", grouped["w6"], 256, 384)
-        quantize("w6", grouped["w6"], 384, 512)
-        z_chunk(3, 3)
-        z_chunk(0, 4)
-        close_group("g", 2, "w4", "s")
-        quantize("z", z_bf, 256, 512)
-        quantize("z", z_bf, 0, 256)
-        quantize("g", g_bf, 256, 512)
-        out_acc[0, 0] = bank(0, [P, 256])
-        product(out_acc[0, 0][:], "w5", 0, codes["z"], scales["z"], slice(0, 256), True, False)
-        out_acc[1, 0] = bank(5, [P, 256])
-        product(out_acc[1, 0][:], "w5", 1, codes["z"], scales["z"], slice(0, 256), True, False)
-        out_acc[2, 0] = bank(1, [P, 256])
-        product(out_acc[2, 0][:], "w5", 2, codes["z"], scales["z"], slice(0, 256), True, False)
-        out_acc[3, 0] = bank(2, [P, 256])
-        product(out_acc[3, 0][:], "w5", 3, codes["z"], scales["z"], slice(0, 256), True, False)
-        out_acc[0, 256] = bank(6, [P, 256])
-        product(out_acc[0, 256][:], "w5", 0, codes["z"], scales["z"], slice(256, 512), True, False)
-        out_acc[1, 256] = bank(3, [P, 256])
-        product(out_acc[1, 256][:], "w5", 1, codes["z"], scales["z"], slice(256, 512), True, False)
-        out_acc[2, 256] = bank(4, [P, 256])
-        product(out_acc[2, 256][:], "w5", 2, codes["z"], scales["z"], slice(256, 512), True, False)
-        out_acc[3, 256] = bank(7, [P, 256])
-        product(out_acc[3, 256][:], "w5", 3, codes["z"], scales["z"], slice(256, 512), True, False)
-        product(out_acc[0, 256][:], "w6", 0, codes["g"], scales["g"], slice(256, 512), False, True)
-        product(out_acc[1, 256][:], "w6", 1, codes["g"], scales["g"], slice(256, 512), False, True)
-        product(out_acc[2, 256][:], "w6", 2, codes["g"], scales["g"], slice(256, 512), False, True)
-        product(out_acc[3, 256][:], "w6", 3, codes["g"], scales["g"], slice(256, 512), False, True)
-        product(out_acc[0, 0][:], "w6", 0, codes["g"], scales["g"], slice(0, 256), False, True)
-        product(out_acc[1, 0][:], "w6", 1, codes["g"], scales["g"], slice(0, 256), False, True)
-        product(out_acc[2, 0][:], "w6", 2, codes["g"], scales["g"], slice(0, 256), False, True)
-        product(out_acc[3, 0][:], "w6", 3, codes["g"], scales["g"], slice(0, 256), False, True)
-        copy("v", out_half[1][:, 0, 0:256], out_acc[0, 256][:])
-        copy("s", out_half[1][:, 1, 0:256], out_acc[1, 256][:])
-        copy("v", out_half[1][:, 2, 0:256], out_acc[2, 256][:])
-        copy("s", out_half[1][:, 3, 0:256], out_acc[3, 256][:])
-        nc.sync.dma_start(out=out_rows[:, 0:4, 256:512], in_=out_half[1][:, 0:4, 0:256])
-        copy("s", out_half[0][:, 0, 0:256], out_acc[0, 0][:])
-        copy("s", out_half[0][:, 1, 0:256], out_acc[1, 0][:])
-        copy("v", out_half[0][:, 2, 0:256], out_acc[2, 0][:])
-        copy("s", out_half[0][:, 3, 0:256], out_acc[3, 0][:])
-        nc.sync.dma_start(out=out_rows[:, 0:4, 0:256], in_=out_half[0][:, 0:4, 0:256])
-        weave_out("v", 0, 256)
-        quantize("out", out_bf, 0, 256)
-        nc.sync.dma_start(out=out_words[:, 0:256], in_=codes["out"][:, 0:256].bitcast(I32))
-        weave_out("v", 256, 384)
-        weave_out("s", 384, 512)
-        quantize("out", out_bf, 256, 512)
-        nc.sync.dma_start(out=out_words[:, 256:512], in_=codes["out"][:, 256:512].bitcast(I32))
-        nc.scalar.dma_start(out=out_2[0, 0:4, :].bitcast(I32), in_=scales["out"][0:4, :].bitcast(I32))
-        nc.sync.dma_start(out=out_2[0, 4:8, :].bitcast(I32), in_=scales["out"][32:36, :].bitcast(I32))
-        nc.scalar.dma_start(out=out_2[0, 8:12, :].bitcast(I32), in_=scales["out"][64:68, :].bitcast(I32))
-        nc.sync.dma_start(out=out_2[0, 12:16, :].bitcast(I32), in_=scales["out"][96:100, :].bitcast(I32))
+        def out_passes(h, weight, moving, start, stop):
+            for t in range(PACK):
+                product(out_banks[h][t][:], weight, t, moving, halves[h], start, stop)
+
+        def empty_and_store(h):
+            for t in range(PACK):
+                copy = vector_copy if EMPTIED_BY[h][t] == "v" else scalar_copy
+                copy(out=out_halves[h][:, t, :], in_=out_banks[h][t][:])
+                if (t + 1) % STORE_GROUPS[h] == 0:
+                    done = slice(t + 1 - STORE_GROUPS[h], t + 1)
+                    nc.sync.dma_start(out=out_rows[:, done, halves[h]], in_=out_halves[h][:, done, :])
+
+        out_passes(0, "w5", "z", True, False)
+        out_passes(1, "w5", "z", True, False)
+        for h in range(2):
+            out_passes(h, "w6", "g", False, True)
+            empty_and_store(h)
+
+        def weave_out(h, copy, c0, c1):
+            src = out_halves[h][:, :, c0:c1].rearrange("p t (c i) -> p c t i", i=4)
+            dst = woven["out"][:, PACK * (HALF * h + c0) : PACK * (HALF * h + c1)]
+            copy(out=dst.rearrange("p (c i t) -> p c t i", i=4, t=PACK), in_=src)
+
+        out_words = out_1[0].rearrange("p n t -> p (n t)").bitcast(I32)
+        for h, cols in enumerate(halves):
+            weave_out(h, vector_copy, 0, VECTOR_WEAVES[h])
+            if VECTOR_WEAVES[h] < HALF:
+                weave_out(h, scalar_copy, VECTOR_WEAVES[h], HALF)
+            quantize("out", cols.start, cols.stop)
+            nc.sync.dma_start(out=out_words[:, cols], in_=words["out"][:, cols].bitcast(I32))
+        for q in range(QUADRANTS):
+            (nc.sync if q % 2 else nc.scalar).dma_start(
+                out=out_2[0, 4 * q : 4 * q + 4, :].bitcast(I32),
+                in_=scales["out"][32 * q : 32 * q + 4, :].bitcast(I32),
+            )

@@ -92,9 +92,11 @@ def tile_picked_zspan_none_po_kernel(
             copy(out=dst[:, m0:m1, :, t0:t1], in_=src[:, m0 - h * per : m1 - h * per, :, t0:t1])
 
         def round_on_vector(name):
-            per = P // PIECES[name]
-            for m0 in range(0, P, per):
-                round_part(name, vector_copy, m0, m0 + per, 0, PACK)
+            per = P // PIECES[name] // 2
+            dst = woven[name][:].rearrange("p (t a r j) -> p a j r t", t=PACK, r=2, j=PACK)
+            for h in range(PIECES[name]):
+                src = raw[name][h][:].rearrange("p j (a r t) -> p a j r t", r=2, t=PACK)
+                nc.vector.tensor_copy(out=dst[:, h * per : (h + 1) * per], in_=src)
 
         def round_shared(name):
             share = SCALAR_SHARE[name]

from contextlib import ExitStack

import concourse.mybir as mybir

TOKENS = 1024
SPANS = 512
WIDTH = 512
FLOPS = 6 * 2 * WIDTH * WIDTH * SPANS

F32 = mybir.dt.float32
BF16 = mybir.dt.bfloat16
I32 = mybir.dt.int32
U32 = mybir.dt.uint32
U16 = mybir.dt.uint16
U8 = mybir.dt.uint8
FP8X4 = mybir.dt.float8_e4m3fn_x4
RELU = mybir.ActivationFunctionType.Relu
MULT = mybir.AluOpType.mult

P = 128
PACK = 4
QUADRANTS = 4
CHUNK = 128
CHUNKS = SPANS // CHUNK
HALF = SPANS // 2

PIECES = {"w1": 1, "w2": 1, "w3": 2, "w4": 1, "w5": 1, "w6": 2}
SCALAR_SHARE = {"w1": 64, "w2": 0, "w4": 96, "w5": 64}
VECTOR_WEAVES = (256, 160)
EMPTIED_BY = ("svsv", "svss")
STORE_GROUPS = (2, 4)


def tile_picked_zspan_none_po_kernel(
    tc, x_words, x_scales, w1, w2, w3, w4, w5, w6, offs, end, out_0, out_1, out_2
):
    nc = tc.nc
    vector_copy = nc.vector.tensor_copy
    scalar_copy = nc.scalar.copy

    with ExitStack() as ctx:
        lists = ctx.enter_context(tc.tile_pool(name="lists", bufs=1))
        keep = ctx.enter_context(tc.tile_pool(name="keep", bufs=1))
        psum = ctx.enter_context(tc.psum_pool(name="psum", bufs=1))

        def sbuf(name, shape, dtype):
            return keep.tile(shape, dtype, name=name, align_bytes=64)

        def bank(b, shape):
            return psum.tile(shape, F32, name="bank%d" % b, tag="bank%d" % b)

        list_tiles = {side: lists.tile([P, SPANS // 16], U16, name="list_" + side) for side in ("start", "end")}
        table_scales = sbuf("table_scales", [P, TOKENS], U8)
        table_words = sbuf("table_words", [P, TOKENS], U32)
        weights = {"w1": w1, "w2": w2, "w3": w3, "w4": w4, "w5": w5, "w6": w6}
        raw = {name: [] for name in weights}

        def load_piece(name, h):
            width = WIDTH // PIECES[name]
            piece = sbuf("raw_%s_%d" % (name, h), [P, PACK, width], F32)
            rows = weights[name].rearrange("(p j) c -> p j c", j=PACK)
            nc.sync.dma_start(out=piece[:], in_=rows[:, :, h * width : (h + 1) * width])
            raw[name].append(piece)

        nc.sync.dma_start(list_tiles["start"][:], offs)
        for q in range(QUADRANTS):
            (nc.scalar if q < QUADRANTS // 2 else nc.sync).dma_start(
                out=table_scales[32 * q : 32 * q + 32, :].bitcast(I32),
                in_=x_scales[0, 4 * q : 4 * q + 4, :].bitcast(I32).partition_broadcast(8),
            )
        nc.sync.dma_start(list_tiles["end"][:], end)
        zero = sbuf("zero", [P, 1], F32)
        nc.vector.memset(zero[:], 0.0)
        zero_bias = sbuf("zero_bias", [P, 1], F32)
        nc.scalar.activation(out=zero_bias[:], in_=zero[:], func=RELU)

        nc.sync.dma_start(out=table_words[:].bitcast(I32), in_=x_words[0].rearrange("p n t -> p (n t)").bitcast(I32))
        for name in weights:
            for h in range(PIECES[name]):
                load_piece(name, h)

        made_here = list(weights) + ["z", "g", "out"]
        woven = {name: sbuf("woven_" + name, [P, WIDTH * PACK], BF16) for name in made_here}
        words = {name: sbuf("words_" + name, [P, WIDTH], U32) for name in made_here + ["start", "end"]}
        scales = {name: sbuf("scales_" + name, [P, WIDTH], U8) for name in made_here + ["start", "end"]}

        def round_part(name, copy, m0, m1, t0, t1):
            per = P // PIECES[name]
            h = m0 // per
            src = raw[name][h][:].rearrange("p j (m t) -> p m j t", t=PACK)
            dst = woven[name][:].rearrange("p (t m j) -> p m j t", t=PACK, j=PACK)
            copy(out=dst[:, m0:m1, :, t0:t1], in_=src[:, m0 - h * per : m1 - h * per, :, t0:t1])

        def round_on_vector(name):
            per = P // PIECES[name] // 2
            dst = woven[name][:].rearrange("p (t a r j) -> p a j r t", t=PACK, r=2, j=PACK)
            for h in range(PIECES[name]):
                src = raw[name][h][:].rearrange("p j (a r t) -> p a j r t", r=2, t=PACK)
                nc.vector.tensor_copy(out=dst[:, h * per : (h + 1) * per], in_=src)

        def round_shared(name):
            share = SCALAR_SHARE[name]
            if share:
                round_part(name, scalar_copy, 0, share, 2, PACK)
            round_part(name, vector_copy, share, P, 2, PACK)
            round_part(name, scalar_copy, 0, P, 0, 2)

        def quantize(name, c0=0, c1=WIDTH):
            nc.vector.quantize_mx(
                out=words[name][:, c0:c1].bitcast(FP8X4),
                scales=scales[name][:, c0:c1],
                in_=woven[name][:, PACK * c0 : PACK * c1],
            )

        def quantize_pairs(name, order):
            for pair in order:
                quantize(name, pair * 2 * P, (pair + 1) * 2 * P)

        def product(acc, weight, t, moving, cols, start, stop):
            group = slice(t * P, (t + 1) * P)
            nc.tensor.matmul_mx(
                out=acc,
                lhsT=words[weight][:, group].bitcast(FP8X4),
                lhsT_scale=scales[weight][:, group],
                rhs=words[moving][:, cols].bitcast(FP8X4),
                rhs_scale=scales[moving][:, cols],
                start=start,
                stop=stop,
            )

        def chunk_cols(c):
            return slice(c * CHUNK, (c + 1) * CHUNK)

        def weaving_read(acc):
            return acc[:].rearrange("p t n -> p n t")

        def woven_chunk(tile, c):
            return tile[:, PACK * CHUNK * c : PACK * CHUNK * (c + 1)].rearrange("p (n t) -> p n t", t=PACK)

        for side in ("start", "end"):
            nc.vector.tensor_copy(scales[side][:], table_scales[:].indirect(list_tiles[side][:]))
            nc.vector.tensor_copy(words[side][:], table_words[:].indirect(list_tiles[side][:]))

        for name in weights:
            if name in SCALAR_SHARE:
                round_shared(name)
            else:
                round_on_vector(name)
            quantize_pairs(name, (1, 0))

        y_chunks = [sbuf("y_%d" % c, [P, PACK * CHUNK], F32) for c in range(CHUNKS)]
        for c in range(CHUNKS):
            acc = bank(c, [P, PACK, CHUNK])
            for t in range(PACK):
                product(acc[:, t, :], "w1", t, "start", chunk_cols(c), True, True)
            nc.scalar.copy(out=woven_chunk(y_chunks[c], 0), in_=weaving_read(acc))

        g_banks = [bank(CHUNKS + c, [P, PACK, CHUNK]) for c in range(CHUNKS)]
        for c in range(CHUNKS):
            for t in range(PACK):
                product(g_banks[c][:, t, :], "w3", t, "start", chunk_cols(c), t == 0, False)

        for c in range(CHUNKS):
            acc = bank(c, [P, PACK, CHUNK])
            for t in range(PACK):
                product(acc[:, t, :], "w2", t, "end", chunk_cols(c), True, True)
            nc.vector.tensor_tensor(
                out=woven_chunk(woven["z"], c), in0=weaving_read(acc), in1=woven_chunk(y_chunks[c], 0), op=MULT
            )

        halves = [slice(0, HALF), slice(HALF, SPANS)]
        for cols in halves:
            quantize("z", cols.start, cols.stop)

        for c in range(CHUNKS):
            for t in range(PACK):
                product(g_banks[c][:, t, :], "w4", t, "end", chunk_cols(c), False, t == PACK - 1)
            nc.scalar.activation(
                out=woven_chunk(woven["g"], c), in_=weaving_read(g_banks[c]), func=RELU, bias=zero_bias[:]
            )

        for cols in halves:
            quantize("g", cols.start, cols.stop)

        out_banks = [[bank(PACK * h + t, [P, HALF]) for t in range(PACK)] for h in range(2)]
        out_rows = out_0.rearrange("(p t) j -> p t j", t=PACK)
        out_halves = [sbuf("out_f32_%d" % h, [P, PACK, HALF], F32) for h in range(2)]

        def out_passes(h, weight, moving, start, stop):
            for t in range(PACK):
                product(out_banks[h][t][:], weight, t, moving, halves[h], start, stop)

        def empty_and_store(h):
            for t in range(PACK):
                copy = vector_copy if EMPTIED_BY[h][t] == "v" else scalar_copy
                copy(out=out_halves[h][:, t, :], in_=out_banks[h][t][:])
                if (t + 1) % STORE_GROUPS[h] == 0:
                    done = slice(t + 1 - STORE_GROUPS[h], t + 1)
                    nc.sync.dma_start(out=out_rows[:, done, halves[h]], in_=out_halves[h][:, done, :])

        out_passes(0, "w5", "z", True, False)
        out_passes(1, "w5", "z", True, False)
        for h in range(2):
            out_passes(h, "w6", "g", False, True)
            empty_and_store(h)

        def weave_out(h, copy, c0, c1):
            src = out_halves[h][:, :, c0:c1].rearrange("p t (c i) -> p c t i", i=4)
            dst = woven["out"][:, PACK * (HALF * h + c0) : PACK * (HALF * h + c1)]
            copy(out=dst.rearrange("p (c i t) -> p c t i", i=4, t=PACK), in_=src)

        out_words = out_1[0].rearrange("p n t -> p (n t)").bitcast(I32)
        for h, cols in enumerate(halves):
            weave_out(h, vector_copy, 0, VECTOR_WEAVES[h])
            if VECTOR_WEAVES[h] < HALF:
                weave_out(h, scalar_copy, VECTOR_WEAVES[h], HALF)
            quantize("out", cols.start, cols.stop)
            nc.sync.dma_start(out=out_words[:, cols], in_=words["out"][:, cols].bitcast(I32))
        for q in range(QUADRANTS):
            (nc.sync if q % 2 else nc.scalar).dma_start(
                out=out_2[0, 4 * q : 4 * q + 4, :].bitcast(I32),
                in_=scales["out"][32 * q : 32 * q + 4, :].bitcast(I32),
            )
